import numpy as np
import ml_dtypes


def mxq(x, axis, fmt="e4m3"):
    dtype, down = {"e4m3": (ml_dtypes.float8_e4m3fn, 7), "e5m2": (ml_dtypes.float8_e5m2, 14)}[fmt]
    v = np.moveaxis(np.asarray(x, np.float32).astype(ml_dtypes.bfloat16).astype(np.float64), axis, -1)
    blocks = v.reshape(v.shape[:-1] + (-1, 32))
    amax = np.abs(blocks).max(-1, keepdims=True)
    byte = np.maximum(np.where(amax > 0, np.frexp(amax)[1] - 1 + 127, 0) - down, 1)
    scale = np.exp2(byte - 127.0)
    codes = (blocks / scale).astype(np.float32).astype(dtype).astype(np.float64)
    return np.moveaxis((codes * scale).reshape(v.shape), -1, axis)


WIDE = False


def mx_kscale(k):
    if not WIDE:
        return np.ones(k)
    levels = np.array([10, -10, 5, -5, 0])
    if k % 512:
        return np.exp2(np.random.permutation(np.resize(levels, k // 32))).repeat(32)
    a = np.empty((k // 512, 16))
    for p in range(k // 512):
        a[p, :8] = np.random.permutation(np.resize(levels, 8))
        for g in range(8):
            far = levels[np.abs(levels - a[p, g]) >= 10]
            a[p, g + 8] = far[np.random.randint(len(far))]
    return np.exp2(a.ravel()).repeat(32)


def f64(x):
    return np.asarray(x).astype(np.float64)


def striped(idx):
    return np.tile(idx.reshape(-1, 16).T, (8, 1)).astype(np.uint16)


def unstriped(offs):
    return offs[:16].T.reshape(-1).astype(np.int64)


E2M1 = np.array([0.0, 0.5, 1.0, 1.5, 2.0, 3.0, 4.0, 6.0, -0.0, -0.5, -1.0, -1.5, -2.0, -3.0, -4.0, -6.0])


def pack_weight(w, fmt):
    k, n = w.shape
    w = f64(np.asarray(w, np.float32).astype(ml_dtypes.bfloat16)).reshape(k // 32, 32, n)
    amax = np.abs(w).max(1)
    if fmt == "e4m3":
        byte = np.frexp(amax)[1] - 1 + 127 - 7
    else:
        mant, ex = np.frexp(amax / 6.0)
        byte = np.where(mant > 0.5, ex, ex - 1) + 127
    byte = np.clip(np.where(amax > 0, byte, 1), 1, 254)
    scaled = (w * np.exp2(127.0 - byte)[:, None, :]).reshape(k, n).astype(np.float32)
    by_word = np.ascontiguousarray(scaled.reshape(k // 512, 128, 4, n).transpose(0, 1, 3, 2))
    if fmt == "e4m3":
        words = by_word.astype(ml_dtypes.float8_e4m3fn).view(np.uint8)
    else:
        c = by_word.astype(ml_dtypes.float4_e2m1fn).view(np.uint8) & 0xF
        words = (c[..., 0::2] | (c[..., 1::2] << 4)).reshape(k // 512, 128, 2 * n)
    return np.ascontiguousarray(words), np.ascontiguousarray(byte.astype(np.uint8).reshape(k // 512, 16, n))


def unpack_weight(words, scales, fmt):
    g, _, n = scales.shape
    words = np.ascontiguousarray(words).reshape(g, 128, n, -1)
    if fmt == "e4m3":
        vals = words.view(ml_dtypes.float8_e4m3fn).astype(np.float64)
    else:
        nib = np.empty((g, 128, n, 4), np.uint8)
        nib[..., 0::2] = words & 0xF
        nib[..., 1::2] = words >> 4
        vals = E2M1[nib]
    vals = vals * np.repeat(np.exp2(scales.astype(np.float64) - 127.0), 8, axis=1)[..., None]
    return vals.transpose(0, 1, 3, 2).reshape(g * 512, n)


K, T, E, C, N = 2560, 768, 6, 128, 128
K8 = 1024


def by_expert(wq, xq):
    return np.concatenate([wq[e].T @ xq[:, e * C:(e + 1) * C] for e in range(E)], axis=1)


def setup_inputs():
    n = np.random.standard_normal
    s = mx_kscale(K)[:, None]
    w = n((E, K, N)) / np.sqrt(K) / s[None]
    w8 = [pack_weight(m[:K8], "e4m3") for m in w]
    w4 = [pack_weight(m[K8:], "e2m1") for m in w]
    return {
        "xT": (n((K, T)) * s).astype(np.float32),
        "w8_words": np.stack([m[0] for m in w8]),
        "w8_scales": np.stack([m[1] for m in w8]),
        "w4_words": np.stack([m[0] for m in w4]),
        "w4_scales": np.stack([m[1] for m in w4]),
        "gate": np.tile(np.random.uniform(0.2, 1.0, E * C), (N, 1)).astype(np.float32),
        "offs": striped(np.random.permutation(T)[:E * C]),
        "dst": striped(np.random.permutation(T)[:E * C]),
    }


def reference(xT, w8_words, w8_scales, w4_words, w4_scales, gate, offs, dst):
    idx = unstriped(offs)
    w = np.stack([np.concatenate([unpack_weight(w8_words[e], w8_scales[e], "e4m3"), unpack_weight(w4_words[e], w4_scales[e], "e2m1")]) for e in range(E)])
    xq = mxq(f64(xT)[:, idx], 0, "e4m3")
    y = by_expert(w, xq)
    out = np.zeros((N, T))
    out[:, unstriped(dst)] = f64(gate) * y
    return out

@@ -1,0 +1,157 @@
+from contextlib import ExitStack
+
+import concourse.mybir as mybir
+
+K, T, E, C, N = 2560, 768, 6, 128, 128
+P = 128
+PASSES = 5
+PASSES8 = 2
+FLOPS = 2 * K * N * E * C
+
+F32 = mybir.dt.float32
+BF16 = mybir.dt.bfloat16
+I32 = mybir.dt.int32
+U32 = mybir.dt.uint32
+U16 = mybir.dt.uint16
+U8 = mybir.dt.uint8
+FP8X4 = mybir.dt.float8_e4m3fn_x4
+FP4X4 = mybir.dt.float4_e2m1fn_x4
+MULT = mybir.AluOpType.mult
+COPY = mybir.ActivationFunctionType.Copy
+
+LOADS = [(0, 512), (512, 768)]
+COPIES = {
+    0: [(0, 352, True), (352, 512, False), (512, 688, True), (688, 768, False)],
+    1: [(0, 512, False), (512, 640, False), (640, 768, True)],
+    2: [(0, 512, False), (512, 640, False), (640, 768, True)],
+    3: [(0, 512, False), (512, 640, False), (640, 768, True)],
+    4: [(0, 320, False), (320, 512, True), (512, 608, False), (608, 768, True)],
+}
+QUANT = [(0, 512), (512, 768)]
+PLANE = {0: (0, 4), 1: (0, 8), 2: (0, 0), 3: (0, 12), 4: (1, 0)}
+W = 1024
+HALF = E * C // 2
+HCOL = HALF // 16
+
+
+def tile_moe_two_lin_none_kernel(tc, xT, w8_words, w8_scales, w4_words, w4_scales, gate, offs, dst, out):
+    nc = tc.nc
+    with ExitStack() as ctx:
+        keep = ctx.enter_context(tc.tile_pool(name="keep", bufs=1))
+        psum = ctx.enter_context(tc.psum_pool(name="psum", bufs=1))
+
+        offs_t = keep.tile([P, T // 16], U16, name="offs_t")
+        dst_t = keep.tile([P, T // 16], U16, name="dst_t")
+        w8 = keep.tile([P, E * 2, 4 * N], U8, name="w8", align_bytes=256)
+        w4 = keep.tile([P, E * 3, 2 * N], U8, name="w4", align_bytes=256)
+        ws = keep.tile([P, E * PASSES, N], U8, name="ws", align_bytes=256)
+        ws_in = keep.tile([16, E * PASSES, N], U8, name="ws_in", align_bytes=256)
+        gate_t = keep.tile([P, E * C], F32, name="gate_t")
+        y = keep.tile([P, E * C], F32, name="y")
+        placed = keep.tile([P, T], F32, name="placed")
+        codes = [keep.tile([P, W], I32, name=f"codes{a}", align_bytes=256) for a in range(PASSES)]
+        scales = [keep.tile([P, W], U8, name=f"scales{i}", align_bytes=256) for i in range(2)]
+        gcodes = [keep.tile([P, E * C], U32, name=f"gcodes{a}", align_bytes=256) for a in range(PASSES)]
+        gscales = [keep.tile([P, E * C], U8, name=f"gscales{i}", align_bytes=256) for i in range(2)]
+        moved = keep.tile([P, E * C], U8, name="moved", align_bytes=256)
+        grouped = [keep.tile([P, T, 4], BF16, name=f"grouped{a}", align_bytes=256) for a in range(PASSES)]
+        raw = {a: [keep.tile([P, 4, hi - lo], F32, name=f"raw{a}_{lo}") for lo, hi in LOADS] for a in range(PASSES)}
+        acc = [psum.tile([N, 512], F32, name=f"acc{e}") for e in range(E)]
+
+        w8_dram = w8_words.bitcast(I32).rearrange("e a p n u -> p (e a) (n u)")
+        w4_dram = w4_words.bitcast(I32).rearrange("e a p m -> p (e a) m")
+        w8s_dram = w8_scales.bitcast(I32).rearrange("e a q n -> q (e a) n")
+        w4s_dram = w4_scales.bitcast(I32).rearrange("e a q n -> q (e a) n")
+
+        def load_x(a):
+            rows = xT[512 * a : 512 * (a + 1), :].rearrange("(p t) w -> p t w", t=4)
+            for tile, (lo, hi) in zip(raw[a], LOADS):
+                nc.sync.dma_start(out=tile[:], in_=rows[:, :, lo:hi])
+
+        load_x(0)
+        nc.sync.dma_start(offs_t[:], offs)
+        for a in range(1, 4):
+            load_x(a)
+        nc.sync.dma_start(out=ws_in[:, 0 : 2 * E, :].bitcast(I32), in_=w8s_dram)
+        nc.sync.dma_start(out=ws_in[:, 2 * E :, :].bitcast(I32), in_=w4s_dram)
+        load_x(4)
+        nc.vector.memset(ws[:].rearrange("p e n -> p (e n)").bitcast(I32), 0)
+        for quad in range(4):
+            nc.sync.dma_start(out=ws[32 * quad : 32 * quad + 4, :, :].bitcast(I32), in_=ws_in[4 * quad : 4 * quad + 4, :, :].bitcast(I32))
+        for h in range(2):
+            nc.sync.dma_start(out=w8[:, 6 * h : 6 * h + 6, :].bitcast(I32), in_=w8_dram[:, 6 * h : 6 * h + 6, :])
+            nc.sync.dma_start(out=w4[:, 9 * h : 9 * h + 9, :].bitcast(I32), in_=w4_dram[:, 9 * h : 9 * h + 9, :])
+            if h == 0:
+                nc.sync.dma_start(out=gate_t[:], in_=gate)
+        nc.sync.dma_start(dst_t[:], dst)
+
+        for i in range(2):
+            nc.vector.memset(scales[i][:].bitcast(I32), 0)
+        for a in range(PASSES):
+            nc.vector.memset(codes[a][:, T:W], 0)
+        nc.gpsimd.memset(moved[:].bitcast(I32), 0)
+
+        def interleave(a):
+            for lo, hi, on_vector in COPIES[a]:
+                tile, first = [(t, l) for t, (l, h) in zip(raw[a], LOADS) if l <= lo and hi <= h][0]
+                src = tile[:, :, lo - first : hi - first].rearrange("p t (c i) -> p c t i", i=4)
+                dest = grouped[a][:, lo:hi, :].rearrange("p (c i) t -> p c t i", i=4)
+                if on_vector:
+                    nc.vector.tensor_copy(dest, src)
+                else:
+                    nc.scalar.activation(dest, src, COPY)
+
+        def quantize(a):
+            i, k = PLANE[a]
+            for lo, hi in QUANT:
+                nc.vector.quantize_mx(
+                    out=codes[a][:, lo:hi].bitcast(FP8X4),
+                    scales=scales[i][k:P, lo:hi],
+                    in_=grouped[a][:, lo:hi, :].rearrange("p w t -> p (w t)"),
+                )
+
+        def gather_codes(a, h):
+            nc.vector.tensor_copy(gcodes[a][:, HALF * h : HALF * (h + 1)], codes[a][:].bitcast(U32).indirect(offs_t[:, HCOL * h : HCOL * (h + 1)]))
+
+        def gather_scales(i, h):
+            nc.vector.tensor_copy(gscales[i][:, HALF * h : HALF * (h + 1)], scales[i][:].indirect(offs_t[:, HCOL * h : HCOL * (h + 1)]))
+
+        def multiply(a, e):
+            i, k = PLANE[a]
+            cols = slice(C * e, C * (e + 1))
+            if a < PASSES8:
+                lhsT, lhsT_scale = w8[:, 2 * e + a, :].bitcast(FP8X4), ws[:, 2 * e + a, :]
+            else:
+                lhsT, lhsT_scale = w4[:, 3 * e + a - 2, :].bitcast(FP4X4), ws[:, 2 * E + 3 * e + a - 2, :]
+            nc.tensor.matmul_mx(
+                out=acc[e][:, 0:C],
+                lhsT=lhsT,
+                lhsT_scale=lhsT_scale,
+                rhs=gcodes[a][:, cols].bitcast(FP8X4),
+                rhs_scale=moved[:, cols] if a == 3 else gscales[i][k:P, cols],
+                start=(a == 0),
+                stop=(a == PASSES - 1),
+            )
+
+        for a in range(4):
+            interleave(a)
+            quantize(a)
+            nc.vector.tensor_copy(gcodes[a][:], codes[a][:].bitcast(U32).indirect(offs_t[:]))
+        nc.vector.tensor_copy(gscales[0][:], scales[0][:].indirect(offs_t[:]))
+        for quad in range(4):
+            nc.sync.dma_start(out=moved[32 * quad : 32 * quad + 4, :].bitcast(I32), in_=gscales[0][32 * quad + 12 : 32 * quad + 16, :].bitcast(I32))
+        interleave(4)
+        quantize(4)
+        for h in range(2):
+            gather_codes(4, h)
+            gather_scales(1, h)
+            for e in range(3 * h, 3 * h + 3):
+                for a in range(PASSES):
+                    multiply(a, e)
+        for h in range(2):
+            for e in range(3 * h, 3 * h + 3):
+                cols = slice(C * e, C * (e + 1))
+                nc.scalar.activation(y[:, cols], acc[e][:, 0:C], COPY)
+            half = slice(HALF * h, HALF * (h + 1))
+            nc.vector.tensor_tensor(placed[:].indirect(dst_t[:, HCOL * h : HCOL * (h + 1)]), y[:, half], gate_t[:, half], MULT)
+        nc.sync.dma_start(out=out, in_=placed[:])

@@ -19,19 +19,18 @@ FP4X4 = mybir.dt.float4_e2m1fn_x4
 MULT = mybir.AluOpType.mult
 COPY = mybir.ActivationFunctionType.Copy
 
-LOADS = [(0, 512), (512, 768)]
+LOADS = {0: [(0, 512), (512, 768)], 1: [(0, 768)], 2: [(0, 768)], 3: [(0, 768)], 4: [(0, 512), (512, 768)]}
 COPIES = {
-    0: [(0, 352, True), (352, 512, False), (512, 688, True), (688, 768, False)],
-    1: [(0, 512, False), (512, 640, False), (640, 768, True)],
-    2: [(0, 512, False), (512, 640, False), (640, 768, True)],
-    3: [(0, 512, False), (512, 640, False), (640, 768, True)],
-    4: [(0, 320, False), (320, 512, True), (512, 608, False), (608, 768, True)],
+    0: [(0, 160, False), (160, 512, True), (512, 592, False), (592, 768, True)],
+    1: [(0, 512, False), (512, 768, True)],
+    2: [(0, 512, False), (512, 560, False), (560, 768, True)],
+    3: [(0, 512, False), (512, 592, False), (592, 768, True)],
+    4: [(0, 416, False), (416, 512, True), (512, 640, False), (640, 768, True)],
 }
 QUANT = [(0, 512), (512, 768)]
 PLANE = {0: (0, 4), 1: (0, 8), 2: (0, 0), 3: (0, 12), 4: (1, 0)}
 W = 1024
-HALF = E * C // 2
-HCOL = HALF // 16
+PIECES = [(0, 3), (3, 5), (5, 6)]
 
 
 def tile_moe_two_lin_none_kernel(tc, xT, w8_words, w8_scales, w4_words, w4_scales, gate, offs, dst, out):
@@ -48,6 +47,7 @@ def tile_moe_two_lin_none_kernel(tc, xT, w8_words, w8_scales, w4_words, w4_scale
         ws_in = keep.tile([16, E * PASSES, N], U8, name="ws_in", align_bytes=256)
         gate_t = keep.tile([P, E * C], F32, name="gate_t")
         y = keep.tile([P, E * C], F32, name="y")
+        plain = keep.tile([P, 3 * C], F32, name="plain")
         placed = keep.tile([P, T], F32, name="placed")
         codes = [keep.tile([P, W], I32, name=f"codes{a}", align_bytes=256) for a in range(PASSES)]
         scales = [keep.tile([P, W], U8, name=f"scales{i}", align_bytes=256) for i in range(2)]
@@ -55,7 +55,7 @@ def tile_moe_two_lin_none_kernel(tc, xT, w8_words, w8_scales, w4_words, w4_scale
         gscales = [keep.tile([P, E * C], U8, name=f"gscales{i}", align_bytes=256) for i in range(2)]
         moved = keep.tile([P, E * C], U8, name="moved", align_bytes=256)
         grouped = [keep.tile([P, T, 4], BF16, name=f"grouped{a}", align_bytes=256) for a in range(PASSES)]
-        raw = {a: [keep.tile([P, 4, hi - lo], F32, name=f"raw{a}_{lo}") for lo, hi in LOADS] for a in range(PASSES)}
+        raw = {a: [keep.tile([P, 4, hi - lo], F32, name=f"raw{a}_{lo}") for lo, hi in LOADS[a]] for a in range(PASSES)}
         acc = [psum.tile([N, 512], F32, name=f"acc{e}") for e in range(E)]
 
         w8_dram = w8_words.bitcast(I32).rearrange("e a p n u -> p (e a) (n u)")
@@ -65,17 +65,18 @@ def tile_moe_two_lin_none_kernel(tc, xT, w8_words, w8_scales, w4_words, w4_scale
 
         def load_x(a):
             rows = xT[512 * a : 512 * (a + 1), :].rearrange("(p t) w -> p t w", t=4)
-            for tile, (lo, hi) in zip(raw[a], LOADS):
+            for tile, (lo, hi) in zip(raw[a], LOADS[a]):
                 nc.sync.dma_start(out=tile[:], in_=rows[:, :, lo:hi])
 
         load_x(0)
         nc.sync.dma_start(offs_t[:], offs)
+        nc.sync.dma_start(dst_t[:], dst)
         for a in range(1, 4):
             load_x(a)
         nc.sync.dma_start(out=ws_in[:, 0 : 2 * E, :].bitcast(I32), in_=w8s_dram)
         nc.sync.dma_start(out=ws_in[:, 2 * E :, :].bitcast(I32), in_=w4s_dram)
         load_x(4)
-        nc.vector.memset(ws[:].rearrange("p e n -> p (e n)").bitcast(I32), 0)
+        nc.gpsimd.memset(ws[:].rearrange("p e n -> p (e n)").bitcast(I32), 0)
         for quad in range(4):
             nc.sync.dma_start(out=ws[32 * quad : 32 * quad + 4, :, :].bitcast(I32), in_=ws_in[4 * quad : 4 * quad + 4, :, :].bitcast(I32))
         for h in range(2):
@@ -83,17 +84,16 @@ def tile_moe_two_lin_none_kernel(tc, xT, w8_words, w8_scales, w4_words, w4_scale
             nc.sync.dma_start(out=w4[:, 9 * h : 9 * h + 9, :].bitcast(I32), in_=w4_dram[:, 9 * h : 9 * h + 9, :])
             if h == 0:
                 nc.sync.dma_start(out=gate_t[:], in_=gate)
-        nc.sync.dma_start(dst_t[:], dst)
 
         for i in range(2):
-            nc.vector.memset(scales[i][:].bitcast(I32), 0)
+            nc.gpsimd.memset(scales[i][:].bitcast(I32), 0)
         for a in range(PASSES):
             nc.vector.memset(codes[a][:, T:W], 0)
         nc.gpsimd.memset(moved[:].bitcast(I32), 0)
 
         def interleave(a):
             for lo, hi, on_vector in COPIES[a]:
-                tile, first = [(t, l) for t, (l, h) in zip(raw[a], LOADS) if l <= lo and hi <= h][0]
+                tile, first = [(t, l) for t, (l, h) in zip(raw[a], LOADS[a]) if l <= lo and hi <= h][0]
                 src = tile[:, :, lo - first : hi - first].rearrange("p t (c i) -> p c t i", i=4)
                 dest = grouped[a][:, lo:hi, :].rearrange("p (c i) t -> p c t i", i=4)
                 if on_vector:
@@ -110,11 +110,11 @@ def tile_moe_two_lin_none_kernel(tc, xT, w8_words, w8_scales, w4_words, w4_scale
                     in_=grouped[a][:, lo:hi, :].rearrange("p w t -> p (w t)"),
                 )
 
-        def gather_codes(a, h):
-            nc.vector.tensor_copy(gcodes[a][:, HALF * h : HALF * (h + 1)], codes[a][:].bitcast(U32).indirect(offs_t[:, HCOL * h : HCOL * (h + 1)]))
+        def gather_codes(a, lo, hi):
+            nc.vector.tensor_copy(gcodes[a][:, C * lo : C * hi], codes[a][:].bitcast(U32).indirect(offs_t[:, 8 * lo : 8 * hi]))
 
-        def gather_scales(i, h):
-            nc.vector.tensor_copy(gscales[i][:, HALF * h : HALF * (h + 1)], scales[i][:].indirect(offs_t[:, HCOL * h : HCOL * (h + 1)]))
+        def gather_scales(i, lo, hi):
+            nc.vector.tensor_copy(gscales[i][:, C * lo : C * hi], scales[i][:].indirect(offs_t[:, 8 * lo : 8 * hi]))
 
         def multiply(a, e):
             i, k = PLANE[a]
@@ -142,16 +142,21 @@ def tile_moe_two_lin_none_kernel(tc, xT, w8_words, w8_scales, w4_words, w4_scale
             nc.sync.dma_start(out=moved[32 * quad : 32 * quad + 4, :].bitcast(I32), in_=gscales[0][32 * quad + 12 : 32 * quad + 16, :].bitcast(I32))
         interleave(4)
         quantize(4)
-        for h in range(2):
-            gather_codes(4, h)
-            gather_scales(1, h)
-            for e in range(3 * h, 3 * h + 3):
-                for a in range(PASSES):
-                    multiply(a, e)
-        for h in range(2):
-            for e in range(3 * h, 3 * h + 3):
+        for e in range(E):
+            for a in range(4):
+                multiply(a, e)
+        for lo, hi in PIECES:
+            gather_codes(4, lo, hi)
+            gather_scales(1, lo, hi)
+            for e in range(lo, hi):
+                multiply(4, e)
+        for lo, hi in PIECES:
+            for e in range(lo, hi):
                 cols = slice(C * e, C * (e + 1))
-                nc.scalar.activation(y[:, cols], acc[e][:, 0:C], COPY)
-            half = slice(HALF * h, HALF * (h + 1))
-            nc.vector.tensor_tensor(placed[:].indirect(dst_t[:, HCOL * h : HCOL * (h + 1)]), y[:, half], gate_t[:, half], MULT)
+                if e < 3:
+                    nc.scalar.activation(plain[:, cols], acc[e][:, 0:C], COPY)
+                    nc.gpsimd.tensor_tensor(y[:, cols], plain[:, cols], gate_t[:, cols], MULT)
+                else:
+                    nc.vector.tensor_tensor(y[:, cols], acc[e][:, 0:C], gate_t[:, cols], MULT)
+            nc.vector.tensor_copy(placed[:].indirect(dst_t[:, 8 * lo : 8 * hi]), y[:, C * lo : C * hi])
         nc.sync.dma_start(out=out, in_=placed[:])

@@ -19,18 +19,20 @@ FP4X4 = mybir.dt.float4_e2m1fn_x4
 MULT = mybir.AluOpType.mult
 COPY = mybir.ActivationFunctionType.Copy
 
-LOADS = {0: [(0, 512), (512, 768)], 1: [(0, 768)], 2: [(0, 768)], 3: [(0, 768)], 4: [(0, 512), (512, 768)]}
+HALVES, WHOLE = [(0, 512), (512, 768)], [(0, 768)]
+LOADS = {2: HALVES, 3: WHOLE, 0: WHOLE, 1: WHOLE, 4: HALVES}
 COPIES = {
-    0: [(0, 160, False), (160, 512, True), (512, 592, False), (592, 768, True)],
-    1: [(0, 512, False), (512, 768, True)],
-    2: [(0, 512, False), (512, 560, False), (560, 768, True)],
-    3: [(0, 512, False), (512, 592, False), (592, 768, True)],
-    4: [(0, 416, False), (416, 512, True), (512, 640, False), (640, 768, True)],
+    2: [(0, 320, True), (320, 512, False), (512, 672, True), (672, 768, False)],
+    3: [(0, 384, False), (384, 768, True)],
+    0: [(0, 512, False), (512, 768, True)],
+    1: [(0, 512, False), (512, 608, False), (608, 768, True)],
+    4: [(0, 512, False), (512, 640, False), (640, 768, True)],
 }
 QUANT = [(0, 512), (512, 768)]
-PLANE = {0: (0, 4), 1: (0, 8), 2: (0, 0), 3: (0, 12), 4: (1, 0)}
+PLANE = {2: (0, 0), 3: (0, 12), 0: (1, 4), 1: (1, 8), 4: (1, 0)}
+ORDER = [2, 3, 0, 1, 4]
 W = 1024
-PIECES = [(0, 3), (3, 5), (5, 6)]
+PIECES = [(0, 4), (4, 6)]
 
 
 def tile_moe_two_lin_none_kernel(tc, xT, w8_words, w8_scales, w4_words, w4_scales, gate, offs, dst, out):
@@ -47,7 +49,6 @@ def tile_moe_two_lin_none_kernel(tc, xT, w8_words, w8_scales, w4_words, w4_scale
         ws_in = keep.tile([16, E * PASSES, N], U8, name="ws_in", align_bytes=256)
         gate_t = keep.tile([P, E * C], F32, name="gate_t")
         y = keep.tile([P, E * C], F32, name="y")
-        plain = keep.tile([P, 3 * C], F32, name="plain")
         placed = keep.tile([P, T], F32, name="placed")
         codes = [keep.tile([P, W], I32, name=f"codes{a}", align_bytes=256) for a in range(PASSES)]
         scales = [keep.tile([P, W], U8, name=f"scales{i}", align_bytes=256) for i in range(2)]
@@ -68,10 +69,10 @@ def tile_moe_two_lin_none_kernel(tc, xT, w8_words, w8_scales, w4_words, w4_scale
             for tile, (lo, hi) in zip(raw[a], LOADS[a]):
                 nc.sync.dma_start(out=tile[:], in_=rows[:, :, lo:hi])
 
-        load_x(0)
+        load_x(2)
         nc.sync.dma_start(offs_t[:], offs)
         nc.sync.dma_start(dst_t[:], dst)
-        for a in range(1, 4):
+        for a in ORDER[1:4]:
             load_x(a)
         nc.sync.dma_start(out=ws_in[:, 0 : 2 * E, :].bitcast(I32), in_=w8s_dram)
         nc.sync.dma_start(out=ws_in[:, 2 * E :, :].bitcast(I32), in_=w4s_dram)
@@ -80,8 +81,8 @@ def tile_moe_two_lin_none_kernel(tc, xT, w8_words, w8_scales, w4_words, w4_scale
         for quad in range(4):
             nc.sync.dma_start(out=ws[32 * quad : 32 * quad + 4, :, :].bitcast(I32), in_=ws_in[4 * quad : 4 * quad + 4, :, :].bitcast(I32))
         for h in range(2):
-            nc.sync.dma_start(out=w8[:, 6 * h : 6 * h + 6, :].bitcast(I32), in_=w8_dram[:, 6 * h : 6 * h + 6, :])
             nc.sync.dma_start(out=w4[:, 9 * h : 9 * h + 9, :].bitcast(I32), in_=w4_dram[:, 9 * h : 9 * h + 9, :])
+            nc.sync.dma_start(out=w8[:, 6 * h : 6 * h + 6, :].bitcast(I32), in_=w8_dram[:, 6 * h : 6 * h + 6, :])
             if h == 0:
                 nc.sync.dma_start(out=gate_t[:], in_=gate)
 
@@ -129,34 +130,33 @@ def tile_moe_two_lin_none_kernel(tc, xT, w8_words, w8_scales, w4_words, w4_scale
                 lhsT_scale=lhsT_scale,
                 rhs=gcodes[a][:, cols].bitcast(FP8X4),
                 rhs_scale=moved[:, cols] if a == 3 else gscales[i][k:P, cols],
-                start=(a == 0),
-                stop=(a == PASSES - 1),
+                start=(a == 2),
+                stop=(a == 4),
             )
 
-        for a in range(4):
+        for a in ORDER:
             interleave(a)
             quantize(a)
+            if a == 4:
+                break
             nc.vector.tensor_copy(gcodes[a][:], codes[a][:].bitcast(U32).indirect(offs_t[:]))
-        nc.vector.tensor_copy(gscales[0][:], scales[0][:].indirect(offs_t[:]))
-        for quad in range(4):
-            nc.sync.dma_start(out=moved[32 * quad : 32 * quad + 4, :].bitcast(I32), in_=gscales[0][32 * quad + 12 : 32 * quad + 16, :].bitcast(I32))
-        interleave(4)
-        quantize(4)
-        for e in range(E):
-            for a in range(4):
-                multiply(a, e)
+            if a == 3:
+                nc.vector.tensor_copy(gscales[0][:], scales[0][:].indirect(offs_t[:]))
+                for quad in range(4):
+                    nc.gpsimd.dma_start(out=moved[32 * quad : 32 * quad + 4, :].bitcast(I32), in_=gscales[0][32 * quad + 12 : 32 * quad + 16, :].bitcast(I32))
+                for b in (2, 3):
+                    for e in range(E):
+                        multiply(b, e)
         for lo, hi in PIECES:
             gather_codes(4, lo, hi)
             gather_scales(1, lo, hi)
             for e in range(lo, hi):
-                multiply(4, e)
-        for lo, hi in PIECES:
+                for a in (0, 1, 4):
+                    multiply(a, e)
+        for lo, hi in [(0, 3), (3, 6)]:
             for e in range(lo, hi):
                 cols = slice(C * e, C * (e + 1))
-                if e < 3:
-                    nc.scalar.activation(plain[:, cols], acc[e][:, 0:C], COPY)
-                    nc.gpsimd.tensor_tensor(y[:, cols], plain[:, cols], gate_t[:, cols], MULT)
-                else:
-                    nc.vector.tensor_tensor(y[:, cols], acc[e][:, 0:C], gate_t[:, cols], MULT)
-            nc.vector.tensor_copy(placed[:].indirect(dst_t[:, 8 * lo : 8 * hi]), y[:, C * lo : C * hi])
+                nc.scalar.activation(y[:, cols], acc[e][:, 0:C], COPY)
+            cols = slice(C * lo, C * hi)
+            nc.vector.tensor_tensor(placed[:].indirect(dst_t[:, 8 * lo : 8 * hi]), y[:, cols], gate_t[:, cols], MULT)
         nc.sync.dma_start(out=out, in_=placed[:])

@@ -20,19 +20,20 @@ MULT = mybir.AluOpType.mult
 COPY = mybir.ActivationFunctionType.Copy
 
 HALVES, WHOLE = [(0, 512), (512, 768)], [(0, 768)]
-LOADS = {2: HALVES, 3: WHOLE, 0: WHOLE, 1: WHOLE, 4: HALVES}
+LOADS = {2: [(0, 640), (640, 768)], 3: WHOLE, 0: WHOLE, 1: WHOLE, 4: HALVES}
 COPIES = {
-    2: [(0, 320, True), (320, 512, False), (512, 672, True), (672, 768, False)],
-    3: [(0, 384, False), (384, 768, True)],
-    0: [(0, 512, False), (512, 768, True)],
-    1: [(0, 512, False), (512, 608, False), (608, 768, True)],
-    4: [(0, 512, False), (512, 640, False), (640, 768, True)],
+    2: [(0, 256, False), (256, 512, True), (512, 640, True), (640, 672, False), (672, 768, True)],
+    3: [(0, 352, False), (352, 512, True), (512, 768, True)],
+    0: [(0, 512, False), (512, 704, False), (704, 768, True)],
+    1: [(0, 512, False), (512, 704, False), (704, 768, True)],
+    4: [(0, 416, False), (416, 512, True), (512, 704, False), (704, 768, True)],
 }
-QUANT = [(0, 512), (512, 768)]
+QUANT = {a: HALVES for a in range(5)}
+QUANT[2] = [(0, 512), (512, 640), (640, 768)]
 PLANE = {2: (0, 0), 3: (0, 12), 0: (1, 4), 1: (1, 8), 4: (1, 0)}
 ORDER = [2, 3, 0, 1, 4]
 W = 1024
-PIECES = [(0, 4), (4, 6)]
+PIECES = [(0, 3), (3, 6)]
 
 
 def tile_moe_two_lin_none_kernel(tc, xT, w8_words, w8_scales, w4_words, w4_scales, gate, offs, dst, out):
@@ -104,18 +105,22 @@ def tile_moe_two_lin_none_kernel(tc, xT, w8_words, w8_scales, w4_words, w4_scale
 
         def quantize(a):
             i, k = PLANE[a]
-            for lo, hi in QUANT:
+            for lo, hi in QUANT[a]:
                 nc.vector.quantize_mx(
                     out=codes[a][:, lo:hi].bitcast(FP8X4),
                     scales=scales[i][k:P, lo:hi],
                     in_=grouped[a][:, lo:hi, :].rearrange("p w t -> p (w t)"),
                 )
 
-        def gather_codes(a, lo, hi):
-            nc.vector.tensor_copy(gcodes[a][:, C * lo : C * hi], codes[a][:].bitcast(U32).indirect(offs_t[:, 8 * lo : 8 * hi]))
+        def pick(dest, window, lo, hi):
+            cols = slice(C * lo, C * hi)
+            nc.vector.tensor_copy(dest[:, cols], window.indirect(offs_t[:, 8 * lo : 8 * hi]))
 
-        def gather_scales(i, lo, hi):
-            nc.vector.tensor_copy(gscales[i][:, C * lo : C * hi], scales[i][:].indirect(offs_t[:, 8 * lo : 8 * hi]))
+        def pick_codes(a, lo=0, hi=E):
+            pick(gcodes[a], codes[a][:].bitcast(U32), lo, hi)
+
+        def pick_scales(i):
+            pick(gscales[i], scales[i][:], 0, E)
 
         def multiply(a, e):
             i, k = PLANE[a]
@@ -134,24 +139,31 @@ def tile_moe_two_lin_none_kernel(tc, xT, w8_words, w8_scales, w4_words, w4_scale
                 stop=(a == 4),
             )
 
-        for a in ORDER:
-            interleave(a)
-            quantize(a)
-            if a == 4:
-                break
-            nc.vector.tensor_copy(gcodes[a][:], codes[a][:].bitcast(U32).indirect(offs_t[:]))
-            if a == 3:
-                nc.vector.tensor_copy(gscales[0][:], scales[0][:].indirect(offs_t[:]))
-                for quad in range(4):
-                    nc.gpsimd.dma_start(out=moved[32 * quad : 32 * quad + 4, :].bitcast(I32), in_=gscales[0][32 * quad + 12 : 32 * quad + 16, :].bitcast(I32))
-                for b in (2, 3):
-                    for e in range(E):
-                        multiply(b, e)
+        interleave(2)
+        quantize(2)
+        pick_codes(2)
+        interleave(3)
+        quantize(3)
+        pick_codes(3)
+        pick_scales(0)
+        nc.gpsimd.dma_start(out=moved[0:112, :].bitcast(I32), in_=gscales[0][12:124, :].bitcast(I32))
         for lo, hi in PIECES:
-            gather_codes(4, lo, hi)
-            gather_scales(1, lo, hi)
-            for e in range(lo, hi):
-                for a in (0, 1, 4):
+            for a in (2, 3):
+                for e in range(lo, hi):
+                    multiply(a, e)
+        interleave(0)
+        quantize(0)
+        interleave(1)
+        pick_codes(0)
+        quantize(1)
+        interleave(4)
+        pick_codes(1)
+        quantize(4)
+        pick_scales(1)
+        for lo, hi in PIECES:
+            pick_codes(4, lo, hi)
+            for a in (0, 1, 4):
+                for e in range(lo, hi):
                     multiply(a, e)
         for lo, hi in [(0, 3), (3, 6)]:
             for e in range(lo, hi):

from contextlib import ExitStack

import concourse.mybir as mybir

K, T, E, C, N = 2560, 768, 6, 128, 128
P = 128
PASSES = 5
PASSES8 = 2
FLOPS = 2 * K * N * E * C

F32 = mybir.dt.float32
BF16 = mybir.dt.bfloat16
I32 = mybir.dt.int32
U32 = mybir.dt.uint32
U16 = mybir.dt.uint16
U8 = mybir.dt.uint8
FP8X4 = mybir.dt.float8_e4m3fn_x4
FP4X4 = mybir.dt.float4_e2m1fn_x4
MULT = mybir.AluOpType.mult
COPY = mybir.ActivationFunctionType.Copy

HALVES, WHOLE = [(0, 512), (512, 768)], [(0, 768)]
LOADS = {2: [(0, 640), (640, 768)], 3: WHOLE, 0: WHOLE, 1: WHOLE, 4: HALVES}
COPIES = {
    2: [(0, 256, False), (256, 512, True), (512, 640, True), (640, 672, False), (672, 768, True)],
    3: [(0, 352, False), (352, 512, True), (512, 768, True)],
    0: [(0, 512, False), (512, 704, False), (704, 768, True)],
    1: [(0, 512, False), (512, 704, False), (704, 768, True)],
    4: [(0, 416, False), (416, 512, True), (512, 704, False), (704, 768, True)],
}
QUANT = {a: HALVES for a in range(5)}
QUANT[2] = [(0, 512), (512, 640), (640, 768)]
PLANE = {2: (0, 0), 3: (0, 12), 0: (1, 4), 1: (1, 8), 4: (1, 0)}
ORDER = [2, 3, 0, 1, 4]
W = 1024
PIECES = [(0, 3), (3, 6)]


def tile_moe_two_lin_none_kernel(tc, xT, w8_words, w8_scales, w4_words, w4_scales, gate, offs, dst, out):
    nc = tc.nc
    with ExitStack() as ctx:
        keep = ctx.enter_context(tc.tile_pool(name="keep", bufs=1))
        psum = ctx.enter_context(tc.psum_pool(name="psum", bufs=1))

        offs_t = keep.tile([P, T // 16], U16, name="offs_t")
        dst_t = keep.tile([P, T // 16], U16, name="dst_t")
        w8 = keep.tile([P, E * 2, 4 * N], U8, name="w8", align_bytes=256)
        w4 = keep.tile([P, E * 3, 2 * N], U8, name="w4", align_bytes=256)
        ws = keep.tile([P, E * PASSES, N], U8, name="ws", align_bytes=256)
        ws_in = keep.tile([16, E * PASSES, N], U8, name="ws_in", align_bytes=256)
        gate_t = keep.tile([P, E * C], F32, name="gate_t")
        y = keep.tile([P, E * C], F32, name="y")
        placed = keep.tile([P, T], F32, name="placed")
        codes = [keep.tile([P, W], I32, name=f"codes{a}", align_bytes=256) for a in range(PASSES)]
        scales = [keep.tile([P, W], U8, name=f"scales{i}", align_bytes=256) for i in range(2)]
        gcodes = [keep.tile([P, E * C], U32, name=f"gcodes{a}", align_bytes=256) for a in range(PASSES)]
        gscales = [keep.tile([P, E * C], U8, name=f"gscales{i}", align_bytes=256) for i in range(2)]
        moved = keep.tile([P, E * C], U8, name="moved", align_bytes=256)
        grouped = [keep.tile([P, T, 4], BF16, name=f"grouped{a}", align_bytes=256) for a in range(PASSES)]
        raw = {a: [keep.tile([P, 4, hi - lo], F32, name=f"raw{a}_{lo}") for lo, hi in LOADS[a]] for a in range(PASSES)}
        acc = [psum.tile([N, 512], F32, name=f"acc{e}") for e in range(E)]

        w8_dram = w8_words.bitcast(I32).rearrange("e a p n u -> p (e a) (n u)")
        w4_dram = w4_words.bitcast(I32).rearrange("e a p m -> p (e a) m")
        w8s_dram = w8_scales.bitcast(I32).rearrange("e a q n -> q (e a) n")
        w4s_dram = w4_scales.bitcast(I32).rearrange("e a q n -> q (e a) n")

        def load_x(a):
            rows = xT[512 * a : 512 * (a + 1), :].rearrange("(p t) w -> p t w", t=4)
            for tile, (lo, hi) in zip(raw[a], LOADS[a]):
                nc.sync.dma_start(out=tile[:], in_=rows[:, :, lo:hi])

        load_x(2)
        nc.sync.dma_start(offs_t[:], offs)
        nc.sync.dma_start(dst_t[:], dst)
        for a in ORDER[1:4]:
            load_x(a)
        nc.sync.dma_start(out=ws_in[:, 0 : 2 * E, :].bitcast(I32), in_=w8s_dram)
        nc.sync.dma_start(out=ws_in[:, 2 * E :, :].bitcast(I32), in_=w4s_dram)
        load_x(4)
        nc.gpsimd.memset(ws[:].rearrange("p e n -> p (e n)").bitcast(I32), 0)
        for quad in range(4):
            nc.sync.dma_start(out=ws[32 * quad : 32 * quad + 4, :, :].bitcast(I32), in_=ws_in[4 * quad : 4 * quad + 4, :, :].bitcast(I32))
        for h in range(2):
            nc.sync.dma_start(out=w4[:, 9 * h : 9 * h + 9, :].bitcast(I32), in_=w4_dram[:, 9 * h : 9 * h + 9, :])
            nc.sync.dma_start(out=w8[:, 6 * h : 6 * h + 6, :].bitcast(I32), in_=w8_dram[:, 6 * h : 6 * h + 6, :])
            if h == 0:
                nc.sync.dma_start(out=gate_t[:], in_=gate)

        for i in range(2):
            nc.gpsimd.memset(scales[i][:].bitcast(I32), 0)
        for a in range(PASSES):
            nc.vector.memset(codes[a][:, T:W], 0)
        nc.gpsimd.memset(moved[:].bitcast(I32), 0)

        def interleave(a):
            for lo, hi, on_vector in COPIES[a]:
                tile, first = [(t, l) for t, (l, h) in zip(raw[a], LOADS[a]) if l <= lo and hi <= h][0]
                src = tile[:, :, lo - first : hi - first].rearrange("p t (c i) -> p c t i", i=4)
                dest = grouped[a][:, lo:hi, :].rearrange("p (c i) t -> p c t i", i=4)
                if on_vector:
                    nc.vector.tensor_copy(dest, src)
                else:
                    nc.scalar.activation(dest, src, COPY)

        def quantize(a):
            i, k = PLANE[a]
            for lo, hi in QUANT[a]:
                nc.vector.quantize_mx(
                    out=codes[a][:, lo:hi].bitcast(FP8X4),
                    scales=scales[i][k:P, lo:hi],
                    in_=grouped[a][:, lo:hi, :].rearrange("p w t -> p (w t)"),
                )

        def pick(dest, window, lo, hi):
            cols = slice(C * lo, C * hi)
            nc.vector.tensor_copy(dest[:, cols], window.indirect(offs_t[:, 8 * lo : 8 * hi]))

        def pick_codes(a, lo=0, hi=E):
            pick(gcodes[a], codes[a][:].bitcast(U32), lo, hi)

        def pick_scales(i):
            pick(gscales[i], scales[i][:], 0, E)

        def multiply(a, e):
            i, k = PLANE[a]
            cols = slice(C * e, C * (e + 1))
            if a < PASSES8:
                lhsT, lhsT_scale = w8[:, 2 * e + a, :].bitcast(FP8X4), ws[:, 2 * e + a, :]
            else:
                lhsT, lhsT_scale = w4[:, 3 * e + a - 2, :].bitcast(FP4X4), ws[:, 2 * E + 3 * e + a - 2, :]
            nc.tensor.matmul_mx(
                out=acc[e][:, 0:C],
                lhsT=lhsT,
                lhsT_scale=lhsT_scale,
                rhs=gcodes[a][:, cols].bitcast(FP8X4),
                rhs_scale=moved[:, cols] if a == 3 else gscales[i][k:P, cols],
                start=(a == 2),
                stop=(a == 4),
            )

        interleave(2)
        quantize(2)
        pick_codes(2)
        interleave(3)
        quantize(3)
        pick_codes(3)
        pick_scales(0)
        nc.gpsimd.dma_start(out=moved[0:112, :].bitcast(I32), in_=gscales[0][12:124, :].bitcast(I32))
        for lo, hi in PIECES:
            for a in (2, 3):
                for e in range(lo, hi):
                    multiply(a, e)
        interleave(0)
        quantize(0)
        interleave(1)
        pick_codes(0)
        quantize(1)
        interleave(4)
        pick_codes(1)
        quantize(4)
        pick_scales(1)
        for lo, hi in PIECES:
            pick_codes(4, lo, hi)
            for a in (0, 1, 4):
                for e in range(lo, hi):
                    multiply(a, e)
        for lo, hi in [(0, 3), (3, 6)]:
            for e in range(lo, hi):
                cols = slice(C * e, C * (e + 1))
                nc.scalar.activation(y[:, cols], acc[e][:, 0:C], COPY)
            cols = slice(C * lo, C * hi)
            nc.vector.tensor_tensor(placed[:].indirect(dst_t[:, 8 * lo : 8 * hi]), y[:, cols], gate_t[:, cols], MULT)
        nc.sync.dma_start(out=out, in_=placed[:])
